import numpy as np, ml_dtypes
CORES = [23,39,55,63,87,103,111,127,18,34,50,58,82,98,106,122]
N = 16
R = 16
def setup_inputs(rng):
    m = (rng.standard_normal((N, 128, 128), dtype=np.float32) / 11).astype(ml_dtypes.bfloat16)
    q = rng.standard_normal((128, R), dtype=np.float32).astype(ml_dtypes.bfloat16)
    return {"m": m, "mt": m.transpose(0, 2, 1).copy(), "q": np.broadcast_to(q, (N, 128, R)).copy()}
def setup_inputs_big(rng):
    d = setup_inputs(rng)
    for k in ("m", "mt", "q"): d[k] = (d[k].astype(np.float32) * 1024.0).astype(d[k].dtype)
    return d
def setup_inputs_small(rng):
    d = setup_inputs(rng)
    for k in ("m", "mt", "q"): d[k] = (d[k].astype(np.float32) * (1 / 1024.0)).astype(d[k].dtype)
    return d
def setup_inputs_apart(rng):
    d = setup_inputs(rng)
    f = (10.0 ** rng.permutation(np.linspace(-1.5, 1.5, N))).astype(np.float32).reshape(N, 1, 1)
    for k in ("m", "mt"): d[k] = (d[k].astype(np.float32) * f).astype(d[k].dtype)
    return d
def tie_inputs(x):
    x = dict(x)
    x["mt"] = x["m"].transpose(0, 2, 1).copy(); x["q"] = np.broadcast_to(x["q"][0], x["q"].shape).copy()
    return x
def reference(m, mt, q):
    M, MT, Q = m.astype(np.float64), mt.astype(np.float64), q.astype(np.float64)
    p = sum(MT[j].T @ Q[j] for j in range(N))
    q2 = sum(M[j].T @ p for j in range(N))
    return {"p": np.broadcast_to(p.astype(ml_dtypes.bfloat16 if m.dtype != np.float64 else np.float64), (N, 128, R)), "q2": np.broadcast_to(q2.astype(ml_dtypes.bfloat16 if m.dtype != np.float64 else np.float64), (N, 128, R))}

@@ -1,0 +1,173 @@
+from concourse.bass import DstId, RemoteDMATransfer
+from concourse.mybir import AluOpType
+
+N = 16
+D = 128
+R = 16
+NBLK = 4
+ROWS = D // NBLK
+PPS = D // N
+J = ROWS // PPS
+
+BF, F32 = "bfloat16", "float32"
+SCRATCH = {
+    "msend": ("dram", [NBLK, 128, ROWS], BF),
+    "land": ("dram", [N, 128, ROWS], BF),
+    "big": ("sbuf", [128, J * D], BF),
+    "z": ("sbuf", [N, ROWS * ROWS], BF),
+    "sel": ("sbuf", [128, J * ROWS], BF),
+    "qs": ("sbuf", [128, R], BF),
+    "st": ("sbuf", [128, D], BF),
+    "sb": ("sbuf", [128, D], BF),
+    "pb": ("sbuf", [128, R], BF),
+    "box": ("sbuf", [128, NBLK, 2 * R], BF),
+    "tmp": ("sbuf", [128, NBLK, 2 * R], F32),
+    "res": ("sbuf", [128, 2 * R], BF),
+    "ps_st": ("psum", [128, 512], F32),
+    "ps_s": ("psum", [128, 512], F32),
+    "ps_pb": ("psum", [128, 512], F32),
+    "ps_pp": ("psum", [128, 512], F32),
+    "ps_c": ("psum", [128, 512], F32),
+}
+SEMAPHORES = ["ms", "own", "q", "z", "zs", "sel", "arr1", "big", "m_st", "m_s", "c_st", "c_s", "m_pb", "m_pp", "c_pb",
+              "msg", "m_c", "arr2", "add", "res", "st_p", "st_q", "loc"]
+
+
+def _plan(cores, topo):
+    chips = sorted({topo.chip(c) for c in cores})
+
+    def far(a, b):
+        return 0 if (topo.mates(a, b) or topo.same_plane(a, b)) else 1
+
+    def match(rest):
+        if len(rest) < 2:
+            return (0, list(rest))
+        best = None
+        for b in rest[1:]:
+            sub = match([y for y in rest[1:] if y != b])
+            cost = sub[0] + far(rest[0], b)
+            if best is None or cost < best[0]:
+                best = (cost, [rest[0], b] + sub[1])
+        return best
+
+    seq = [c for ch in match(chips)[1] for c in sorted(cores) if topo.chip(c) == ch]
+    return {c: (i // NBLK, i % NBLK) for i, c in enumerate(seq)}
+
+
+def _bits(mask):
+    return [e for e in range(mask.bit_length()) if (mask >> e) & 1]
+
+
+def _dst(topo, c):
+    rid, pid, _ = topo.addr(c)
+    return DstId(rid=rid, pnc=pid)
+
+
+def rank_program(g, core, T, topo):
+    rank = T.rank_of(core)
+    if rank is None:
+        return
+    sem = T.sem
+    plan = _plan(T.cores, topo)
+    grp, blk = plan[core]
+    others = [c for c in T.cores if c != core]
+    lo, hi = blk * ROWS, (blk + 1) * ROWS
+    pe, ve, sy, sc = g.tensor, g.vector, g.sync, g.scalar
+
+    common = topo.mask(core, others[0])
+    for c in others:
+        common &= topo.mask(core, c)
+    eng = _bits(common)
+    ept = len(eng) // NBLK
+    all_mask = sum(1 << e for e in eng)
+
+    sy.dma_start(T.msend[:], T.m[:]).then_inc(sem.ms, 16)
+    sc.dma_start(T.land[rank], T.m[lo:hi, :]).then_inc(sem.own, 16)
+    sc.dma_start(T.qs[:], T.q[:]).then_inc(sem.q, 16)
+    ve.memset(T.z[:], 0.0).then_inc(sem.z, 1)
+    ve.wait_ge(sem.z, 1)
+    ve.memset(T.z[:, 0:ROWS * ROWS:ROWS + 1], 1.0).then_inc(sem.z, 1)
+    sc.wait_ge(sem.z, 2)
+    sc.dma_start(T.sel[:], T.z[:]).then_inc(sem.sel, 16)
+    nzs = 0
+    if lo > 0:
+        ve.memset(T.st[:, 0:lo], 0.0).then_inc(sem.zs, 1)
+        nzs += 1
+    if hi < D:
+        ve.memset(T.st[:, hi:D], 0.0).then_inc(sem.zs, 1)
+        nzs += 1
+
+    g.wait_ge(sem.ms, 16)
+    trs = []
+    for b in range(NBLK):
+        own = [c for c in others if plan[c][1] == b]
+        trs.append(RemoteDMATransfer(
+            dst_ids=[_dst(topo, c) for c in own],
+            dma_engine_mask=sum(1 << e for e in eng[b * ept:(b + 1) * ept]),
+            remote_sem=sem.arr1, srcs=[T.msend[b]], dsts=[T.land[rank] for _ in own]))
+    g.remote_dma_fused(trs, local_sem=sem.loc)
+    nloc = NBLK * ept
+
+    sy.wait_ge(sem.arr1, (N - 1) * ept)
+    sy.wait_ge(sem.own, 16)
+    sy.dma_start(T.big[:], T.land[:]).then_inc(sem.big, 16)
+
+    pe.wait_ge(sem.big, 16)
+    pe.wait_ge(sem.sel, 16)
+    for j in range(J):
+        i = pe.matmul(T.ps_st[:, 0:ROWS], lhsT=T.big[:, j * D:(j + 1) * D], rhs=T.sel[:, j * ROWS:(j + 1) * ROWS],
+                      start=(j == 0), stop=(j == J - 1))
+    i.then_inc(sem.m_st, 1)
+    for j in range(J):
+        i = pe.matmul(T.ps_s[0:ROWS, 0:D], lhsT=T.sel[:, j * ROWS:(j + 1) * ROWS], rhs=T.big[:, j * D:(j + 1) * D],
+                      start=(j == 0), stop=(j == J - 1))
+    i.then_inc(sem.m_s, 1)
+    ve.wait_ge(sem.m_st, 1)
+    ve.tensor_copy(T.st[:, lo:hi], T.ps_st[:, 0:ROWS]).then_inc(sem.c_st, 1)
+    ve.wait_ge(sem.m_s, 1)
+    ve.tensor_copy(T.sb[0:ROWS, :], T.ps_s[0:ROWS, 0:D]).then_inc(sem.c_s, 1)
+
+    pe.wait_ge(sem.c_st, 1)
+    pe.wait_ge(sem.q, 16)
+    pe.matmul(T.ps_pb[0:ROWS, 0:R], lhsT=T.st[:, lo:hi], rhs=T.qs[:], start=True, stop=True).then_inc(sem.m_pb, 1)
+    pe.wait_ge(sem.zs, nzs)
+    pe.matmul(T.ps_pp[:, 0:R], lhsT=T.st[:], rhs=T.qs[:], start=True, stop=True).then_inc(sem.m_pp, 1)
+    ve.wait_ge(sem.m_pb, 1)
+    ve.tensor_copy(T.pb[0:ROWS, :], T.ps_pb[0:ROWS, 0:R]).then_inc(sem.c_pb, 1)
+    ve.wait_ge(sem.m_pp, 1)
+    ve.tensor_copy(T.box[:, blk, 0:R], T.ps_pp[:, 0:R]).then_inc(sem.msg, 1)
+
+    pe.wait_ge(sem.c_s, 1)
+    pe.wait_ge(sem.c_pb, 1)
+    pe.matmul(T.ps_c[:, 0:R], lhsT=T.sb[0:ROWS, :], rhs=T.pb[0:ROWS, :], start=True, stop=True).then_inc(sem.m_c, 1)
+    ve.wait_ge(sem.m_c, 1)
+    ve.tensor_copy(T.box[:, blk, R:2 * R], T.ps_c[:, 0:R]).then_inc(sem.msg, 1)
+
+    peers = [c for c in others if plan[c][0] == grp]
+    g.wait_ge(sem.msg, 2)
+    g.remote_dma_fused([RemoteDMATransfer(
+        dst_ids=[_dst(topo, c) for c in peers], dma_engine_mask=all_mask, remote_sem=sem.arr2,
+        srcs=[T.box[:, blk, :]], dsts=[T.box[:, blk, :] for _ in peers])], local_sem=sem.loc)
+    nloc += len(eng)
+
+    ve.wait_ge(sem.arr2, len(peers) * len(eng))
+    ve.wait_ge(sem.msg, 2)
+    src, base, n, nadd = T.box, 0, NBLK, 0
+    off = 0
+    while n > 2:
+        h = n // 2
+        ve.tensor_tensor(T.tmp[:, off:off + h, :], src[:, base:base + h, :], src[:, base + h:base + n, :],
+                         AluOpType.add).then_inc(sem.add, 1)
+        nadd += 1
+        ve.wait_ge(sem.add, nadd)
+        src, base, n = T.tmp, off, h
+        off += h
+    ve.tensor_tensor(T.res[:], src[:, base, :], src[:, base + 1, :], AluOpType.add).then_inc(sem.res, 1)
+
+    sy.wait_ge(sem.res, 1)
+    sy.dma_start(T.q2[:], T.res[:, R:2 * R]).then_inc(sem.st_q, 16)
+    sc.wait_ge(sem.res, 1)
+    sc.dma_start(T.p[:], T.res[:, 0:R]).then_inc(sem.st_p, 16)
+    sy.wait_ge(sem.st_q, 16)
+    sc.wait_ge(sem.st_p, 16)
+    g.wait_ge(sem.loc, nloc)

@@ -5,6 +5,7 @@ N = 16
 D = 128
 R = 16
 NBLK = 4
+NGRP = N // NBLK
 ROWS = D // NBLK
 PPS = D // N
 J = ROWS // PPS
@@ -29,8 +30,8 @@ SCRATCH = {
     "ps_pp": ("psum", [128, 512], F32),
     "ps_c": ("psum", [128, 512], F32),
 }
-SEMAPHORES = ["ms", "own", "q", "z", "zs", "sel", "arr1", "big", "m_st", "m_s", "c_st", "c_s", "m_pb", "m_pp", "c_pb",
-              "msg", "m_c", "arr2", "add", "res", "st_p", "st_q", "loc"]
+SEMAPHORES = ["ms", "own", "q", "z", "zs", "sel", "big", "m_st", "m_s", "c_st", "c_s", "m_pb", "m_pp", "c_pb",
+              "msg", "m_c", "arr2", "add", "res", "st_p", "st_q", "loc"] + ["a1_%d" % k for k in range(NGRP)]
 
 
 def _plan(cores, topo):
@@ -70,6 +71,7 @@ def rank_program(g, core, T, topo):
     sem = T.sem
     plan = _plan(T.cores, topo)
     grp, blk = plan[core]
+    slot = grp * NBLK + blk
     others = [c for c in T.cores if c != core]
     lo, hi = blk * ROWS, (blk + 1) * ROWS
     pe, ve, sy, sc = g.tensor, g.vector, g.sync, g.scalar
@@ -82,7 +84,7 @@ def rank_program(g, core, T, topo):
     all_mask = sum(1 << e for e in eng)
 
     sy.dma_start(T.msend[:], T.m[:]).then_inc(sem.ms, 16)
-    sc.dma_start(T.land[rank], T.m[lo:hi, :]).then_inc(sem.own, 16)
+    sc.dma_start(T.land[slot], T.m[lo:hi, :]).then_inc(sem.own, 16)
     sc.dma_start(T.qs[:], T.q[:]).then_inc(sem.q, 16)
     ve.memset(T.z[:], 0.0).then_inc(sem.z, 1)
     ve.wait_ge(sem.z, 1)
@@ -100,19 +102,24 @@ def rank_program(g, core, T, topo):
     g.wait_ge(sem.ms, 16)
     trs = []
     for b in range(NBLK):
-        own = [c for c in others if plan[c][1] == b]
+        own = sorted([c for c in others if plan[c][1] == b], key=lambda c: (plan[c][0] - grp - 1) % NGRP)
         trs.append(RemoteDMATransfer(
             dst_ids=[_dst(topo, c) for c in own],
             dma_engine_mask=sum(1 << e for e in eng[b * ept:(b + 1) * ept]),
-            remote_sem=sem.arr1, srcs=[T.msend[b]], dsts=[T.land[rank] for _ in own]))
+            remote_sem=sem["a1_%d" % grp], srcs=[T.msend[b]], dsts=[T.land[slot] for _ in own]))
     g.remote_dma_fused(trs, local_sem=sem.loc)
     nloc = NBLK * ept
 
-    sy.wait_ge(sem.arr1, (N - 1) * ept)
-    sy.wait_ge(sem.own, 16)
-    sy.dma_start(T.big[:], T.land[:]).then_inc(sem.big, 16)
+    gp = NBLK * PPS
+    for t in range(NGRP):
+        sg = (grp - 1 - t) % NGRP
+        qu = sy if (NGRP - 1 - t) % 2 == 0 else sc
+        qu.wait_ge(sem["a1_%d" % sg], (NBLK - (1 if sg == grp else 0)) * ept)
+        if sg == grp:
+            qu.wait_ge(sem.own, 16)
+        qu.dma_start(T.big[sg * gp:(sg + 1) * gp, :], T.land[sg * NBLK:(sg + 1) * NBLK]).then_inc(sem.big, 16)
 
-    pe.wait_ge(sem.big, 16)
+    pe.wait_ge(sem.big, 16 * NGRP)
     pe.wait_ge(sem.sel, 16)
     for j in range(J):
         i = pe.matmul(T.ps_st[:, 0:ROWS], lhsT=T.big[:, j * D:(j + 1) * D], rhs=T.sel[:, j * ROWS:(j + 1) * ROWS],
@@ -150,6 +157,11 @@ def rank_program(g, core, T, topo):
         srcs=[T.box[:, blk, :]], dsts=[T.box[:, blk, :] for _ in peers])], local_sem=sem.loc)
     nloc += len(eng)
 
+    sc.wait_ge(sem.arr2, len(peers) * len(eng))
+    sc.wait_ge(sem.msg, 2)
+    for b in range(NBLK):
+        sc.dma_start(T.p[b * ROWS:(b + 1) * ROWS, :], T.box[b * ROWS:(b + 1) * ROWS, b, 0:R]).then_inc(sem.st_p, 16)
+
     ve.wait_ge(sem.arr2, len(peers) * len(eng))
     ve.wait_ge(sem.msg, 2)
     src, base, n, nadd = T.box, 0, NBLK, 0
@@ -166,8 +178,6 @@ def rank_program(g, core, T, topo):
 
     sy.wait_ge(sem.res, 1)
     sy.dma_start(T.q2[:], T.res[:, R:2 * R]).then_inc(sem.st_q, 16)
-    sc.wait_ge(sem.res, 1)
-    sc.dma_start(T.p[:], T.res[:, 0:R]).then_inc(sem.st_p, 16)
     sy.wait_ge(sem.st_q, 16)
-    sc.wait_ge(sem.st_p, 16)
+    sc.wait_ge(sem.st_p, 16 * NBLK)
     g.wait_ge(sem.loc, nloc)

@@ -9,29 +9,33 @@ NGRP = N // NBLK
 ROWS = D // NBLK
 PPS = D // N
 J = ROWS // PPS
+GP = NBLK * PPS
+KB = (NGRP - 1) * GP
+H = ROWS // 2
 
 BF, F32 = "bfloat16", "float32"
 SCRATCH = {
     "msend": ("dram", [NBLK, 128, ROWS], BF),
-    "land": ("dram", [N, 128, ROWS], BF),
+    "land": ("dram", [(NGRP - 1) * NBLK, 128, ROWS], BF),
     "big": ("sbuf", [128, J * D], BF),
+    "mts": ("sbuf", [128, D], BF),
+    "dir": ("sbuf", [128, NBLK, ROWS], BF),
     "z": ("sbuf", [N, ROWS * ROWS], BF),
     "sel": ("sbuf", [128, J * ROWS], BF),
-    "qs": ("sbuf", [128, R], BF),
-    "st": ("sbuf", [128, D], BF),
-    "sb": ("sbuf", [128, D], BF),
-    "pb": ("sbuf", [128, R], BF),
+    "idx": ("sbuf", [128, ROWS], BF),
+    "iq": ("sbuf", [128, D + R], BF),
+    "st": ("sbuf", [128, ROWS], BF),
+    "sp": ("sbuf", [128, D + R], BF),
     "box": ("sbuf", [128, NBLK, 2 * R], BF),
-    "tmp": ("sbuf", [128, NBLK, 2 * R], F32),
-    "res": ("sbuf", [128, 2 * R], BF),
+    "acc": ("sbuf", [128, NBLK, R], F32),
+    "res": ("sbuf", [128, R], BF),
     "ps_st": ("psum", [128, 512], F32),
-    "ps_s": ("psum", [128, 512], F32),
-    "ps_pb": ("psum", [128, 512], F32),
-    "ps_pp": ("psum", [128, 512], F32),
+    "ps_sp": ("psum", [128, 512], F32),
     "ps_c": ("psum", [128, 512], F32),
 }
-SEMAPHORES = ["ms", "own", "q", "z", "zs", "sel", "big", "m_st", "m_s", "c_st", "c_s", "m_pb", "m_pp", "c_pb",
-              "msg", "m_c", "arr2", "add", "res", "st_p", "st_q", "loc"] + ["a1_%d" % k for k in range(NGRP)]
+SEMAPHORES = (["ms", "mt", "q", "z", "idn", "idr", "idm", "sel", "big", "m_st", "c_st", "m_sp", "c_sp",
+               "msg", "m_c", "add", "res", "st_p", "st_q", "loc"] + ["a1_%d" % k for k in range(NGRP)]
+              + ["a2_%d" % k for k in range(NBLK)])
 
 
 def _plan(cores, topo):
@@ -59,9 +63,21 @@ def _bits(mask):
     return [e for e in range(mask.bit_length()) if (mask >> e) & 1]
 
 
+def _m(engines):
+    return sum(1 << e for e in engines)
+
+
 def _dst(topo, c):
     rid, pid, _ = topo.addr(c)
     return DstId(rid=rid, pnc=pid)
+
+
+def _order2(c, plan, cores, topo):
+    peers = [x for x in cores if x != c and plan[x][0] == plan[c][0]]
+    near = [x for x in peers if topo.chip(x) == topo.chip(c)]
+    far = sorted(x for x in peers if topo.chip(x) != topo.chip(c))
+    k = sorted([c] + near).index(c) % len(far)
+    return near + far[k:] + far[:k]
 
 
 def rank_program(g, core, T, topo):
@@ -71,8 +87,10 @@ def rank_program(g, core, T, topo):
     sem = T.sem
     plan = _plan(T.cores, topo)
     grp, blk = plan[core]
-    slot = grp * NBLK + blk
     others = [c for c in T.cores if c != core]
+    peers = [c for c in others if plan[c][0] == grp]
+    near = [c for c in peers if topo.chip(c) == topo.chip(core)]
+    far = [c for c in peers if topo.chip(c) != topo.chip(core)]
     lo, hi = blk * ROWS, (blk + 1) * ROWS
     pe, ve, sy, sc = g.tensor, g.vector, g.sync, g.scalar
 
@@ -81,103 +99,132 @@ def rank_program(g, core, T, topo):
         common &= topo.mask(core, c)
     eng = _bits(common)
     ept = len(eng) // NBLK
-    all_mask = sum(1 << e for e in eng)
+    efar = len(eng) // len(far)
+
+    h0 = H * sorted([core] + near).index(core)
+    g.iota(T.idx[:, h0:h0 + H], [[-1, H]], -h0, 1, allow_small_or_imprecise_dtypes=True).then_inc(sem.idn, 1)
+    g.wait_ge(sem.idn, 1)
+    g.remote_dma_fused([RemoteDMATransfer(
+        dst_ids=[_dst(topo, c) for c in near], dma_engine_mask=_m(eng), remote_sem=sem.idr,
+        srcs=[T.idx[:, h0:h0 + H]], dsts=[T.idx[:, h0:h0 + H] for _ in near])], local_sem=sem.loc)
+    nidr = len(eng)
+    nloc = len(eng)
 
     sy.dma_start(T.msend[:], T.m[:]).then_inc(sem.ms, 16)
-    sc.dma_start(T.land[slot], T.m[lo:hi, :]).then_inc(sem.own, 16)
-    sc.dma_start(T.qs[:], T.q[:]).then_inc(sem.q, 16)
+    sy.dma_start(T.mts[:], T.mt[:]).then_inc(sem.mt, 16)
+    sc.dma_start(T.iq[:, D:D + R], T.q[:]).then_inc(sem.q, 16)
     ve.memset(T.z[:], 0.0).then_inc(sem.z, 1)
     ve.wait_ge(sem.z, 1)
     ve.memset(T.z[:, 0:ROWS * ROWS:ROWS + 1], 1.0).then_inc(sem.z, 1)
     sc.wait_ge(sem.z, 2)
     sc.dma_start(T.sel[:], T.z[:]).then_inc(sem.sel, 16)
-    nzs = 0
-    if lo > 0:
-        ve.memset(T.st[:, 0:lo], 0.0).then_inc(sem.zs, 1)
-        nzs += 1
-    if hi < D:
-        ve.memset(T.st[:, hi:D], 0.0).then_inc(sem.zs, 1)
-        nzs += 1
+    nmsg = 0
+    a = ROWS
+    while a < 128:
+        n = a if 2 * a <= 128 else 128 - a
+        ve.memset(T.box[a:a + n, blk, 0:R], 0.0).then_inc(sem.msg, 1)
+        nmsg += 1
+        a += n
+    ve.wait_ge(sem.idn, 1)
+    ve.wait_ge(sem.idr, nidr)
+    for u in range(NBLK):
+        ve.tensor_scalar(T.iq[:, u * ROWS:(u + 1) * ROWS], T.idx[:], float(u * ROWS), None,
+                         AluOpType.is_equal).then_inc(sem.idm, 1)
 
     g.wait_ge(sem.ms, 16)
     trs = []
     for b in range(NBLK):
-        own = sorted([c for c in others if plan[c][1] == b], key=lambda c: (plan[c][0] - grp - 1) % NGRP)
+        own = sorted([c for c in others if plan[c][1] == b and plan[c][0] != grp],
+                     key=lambda c: (plan[c][0] - grp - 1) % NGRP)
         trs.append(RemoteDMATransfer(
-            dst_ids=[_dst(topo, c) for c in own],
-            dma_engine_mask=sum(1 << e for e in eng[b * ept:(b + 1) * ept]),
-            remote_sem=sem["a1_%d" % grp], srcs=[T.msend[b]], dsts=[T.land[slot] for _ in own]))
+            dst_ids=[_dst(topo, c) for c in own], dma_engine_mask=_m(eng[b * ept:(b + 1) * ept]),
+            remote_sem=sem["a1_%d" % grp], srcs=[T.msend[b]],
+            dsts=[T.land[((plan[c][0] - grp - 1) % NGRP) * NBLK + blk] for c in own]))
     g.remote_dma_fused(trs, local_sem=sem.loc)
-    nloc = NBLK * ept
+    nloc += NBLK * ept
 
-    gp = NBLK * PPS
-    for t in range(NGRP):
+    g.wait_ge(sem.mt, 16)
+    trs = []
+    for k, c in enumerate(far):
+        b = plan[c][1]
+        trs.append(RemoteDMATransfer(
+            dst_ids=[_dst(topo, c)], dma_engine_mask=_m(eng[k * efar:(k + 1) * efar]), remote_sem=sem["a1_%d" % grp],
+            srcs=[T.mts[:, b * ROWS:(b + 1) * ROWS]], dsts=[T.dir[:, blk, :]]))
+    g.remote_dma_fused(trs, local_sem=sem.loc)
+    for c in near:
+        b = plan[c][1]
+        g.remote_dma_fused([RemoteDMATransfer(
+            dst_ids=[_dst(topo, c)], dma_engine_mask=_m(eng), remote_sem=sem["a1_%d" % grp],
+            srcs=[T.mts[:, b * ROWS:(b + 1) * ROWS]], dsts=[T.dir[:, blk, :]])], local_sem=sem.loc)
+    ndir = len(far) * efar + len(near) * len(eng)
+    nloc += ndir
+
+    for t in range(NGRP - 1):
         sg = (grp - 1 - t) % NGRP
-        qu = sy if (NGRP - 1 - t) % 2 == 0 else sc
-        qu.wait_ge(sem["a1_%d" % sg], (NBLK - (1 if sg == grp else 0)) * ept)
-        if sg == grp:
-            qu.wait_ge(sem.own, 16)
-        qu.dma_start(T.big[sg * gp:(sg + 1) * gp, :], T.land[sg * NBLK:(sg + 1) * NBLK]).then_inc(sem.big, 16)
+        qu = sy if (NGRP - 2 - t) % 2 == 0 else sc
+        qu.wait_ge(sem["a1_%d" % sg], NBLK * ept)
+        qu.dma_start(T.big[t * GP:(t + 1) * GP, :], T.land[t * NBLK:(t + 1) * NBLK]).then_inc(sem.big, 16)
 
-    pe.wait_ge(sem.big, 16 * NGRP)
+    pe.wait_ge(sem.idm, NBLK)
+    pe.wait_ge(sem.mt, 16)
+    pe.matmul(T.ps_st[:, 0:ROWS], lhsT=T.iq[:, 0:D], rhs=T.mts[:, lo:hi], start=True, stop=False)
+    pe.wait_ge(sem["a1_%d" % grp], ndir)
+    for c in peers:
+        pe.matmul(T.ps_st[:, 0:ROWS], lhsT=T.iq[:, 0:D], rhs=T.dir[:, plan[c][1], :], start=False, stop=False)
+    pe.wait_ge(sem.big, 16 * (NGRP - 1))
     pe.wait_ge(sem.sel, 16)
     for j in range(J):
-        i = pe.matmul(T.ps_st[:, 0:ROWS], lhsT=T.big[:, j * D:(j + 1) * D], rhs=T.sel[:, j * ROWS:(j + 1) * ROWS],
-                      start=(j == 0), stop=(j == J - 1))
+        i = pe.matmul(T.ps_st[:, 0:ROWS], lhsT=T.big[0:KB, j * D:(j + 1) * D],
+                      rhs=T.sel[0:KB, j * ROWS:(j + 1) * ROWS], start=False, stop=(j == J - 1))
     i.then_inc(sem.m_st, 1)
-    for j in range(J):
-        i = pe.matmul(T.ps_s[0:ROWS, 0:D], lhsT=T.sel[:, j * ROWS:(j + 1) * ROWS], rhs=T.big[:, j * D:(j + 1) * D],
-                      start=(j == 0), stop=(j == J - 1))
-    i.then_inc(sem.m_s, 1)
     ve.wait_ge(sem.m_st, 1)
-    ve.tensor_copy(T.st[:, lo:hi], T.ps_st[:, 0:ROWS]).then_inc(sem.c_st, 1)
-    ve.wait_ge(sem.m_s, 1)
-    ve.tensor_copy(T.sb[0:ROWS, :], T.ps_s[0:ROWS, 0:D]).then_inc(sem.c_s, 1)
+    ve.tensor_copy(T.st[:], T.ps_st[:, 0:ROWS]).then_inc(sem.c_st, 1)
 
     pe.wait_ge(sem.c_st, 1)
     pe.wait_ge(sem.q, 16)
-    pe.matmul(T.ps_pb[0:ROWS, 0:R], lhsT=T.st[:, lo:hi], rhs=T.qs[:], start=True, stop=True).then_inc(sem.m_pb, 1)
-    pe.wait_ge(sem.zs, nzs)
-    pe.matmul(T.ps_pp[:, 0:R], lhsT=T.st[:], rhs=T.qs[:], start=True, stop=True).then_inc(sem.m_pp, 1)
-    ve.wait_ge(sem.m_pb, 1)
-    ve.tensor_copy(T.pb[0:ROWS, :], T.ps_pb[0:ROWS, 0:R]).then_inc(sem.c_pb, 1)
-    ve.wait_ge(sem.m_pp, 1)
-    ve.tensor_copy(T.box[:, blk, 0:R], T.ps_pp[:, 0:R]).then_inc(sem.msg, 1)
+    pe.matmul(T.ps_sp[0:ROWS, 0:D + R], lhsT=T.st[:], rhs=T.iq[:], start=True, stop=True).then_inc(sem.m_sp, 1)
+    ve.wait_ge(sem.m_sp, 1)
+    ve.tensor_copy(T.sp[0:ROWS, :], T.ps_sp[0:ROWS, 0:D + R]).then_inc(sem.c_sp, 1)
+    ve.tensor_copy(T.box[0:ROWS, blk, 0:R], T.ps_sp[0:ROWS, D:D + R]).then_inc(sem.msg, 1)
+    nmsg += 1
 
-    pe.wait_ge(sem.c_s, 1)
-    pe.wait_ge(sem.c_pb, 1)
-    pe.matmul(T.ps_c[:, 0:R], lhsT=T.sb[0:ROWS, :], rhs=T.pb[0:ROWS, :], start=True, stop=True).then_inc(sem.m_c, 1)
+    pe.wait_ge(sem.c_sp, 1)
+    pe.matmul(T.ps_c[:, 0:R], lhsT=T.sp[0:ROWS, 0:D], rhs=T.sp[0:ROWS, D:D + R], start=True, stop=True).then_inc(
+        sem.m_c, 1)
     ve.wait_ge(sem.m_c, 1)
     ve.tensor_copy(T.box[:, blk, R:2 * R], T.ps_c[:, 0:R]).then_inc(sem.msg, 1)
+    nmsg += 1
 
-    peers = [c for c in others if plan[c][0] == grp]
-    g.wait_ge(sem.msg, 2)
+    dests = _order2(core, plan, T.cores, topo)
+    g.wait_ge(sem.msg, nmsg)
     g.remote_dma_fused([RemoteDMATransfer(
-        dst_ids=[_dst(topo, c) for c in peers], dma_engine_mask=all_mask, remote_sem=sem.arr2,
-        srcs=[T.box[:, blk, :]], dsts=[T.box[:, blk, :] for _ in peers])], local_sem=sem.loc)
+        dst_ids=[_dst(topo, c) for c in dests], dma_engine_mask=_m(eng), remote_sem=sem["a2_%d" % blk],
+        srcs=[T.box[:, blk, :]], dsts=[T.box[:, blk, :] for _ in dests])], local_sem=sem.loc)
     nloc += len(eng)
 
-    sc.wait_ge(sem.arr2, len(peers) * len(eng))
-    sc.wait_ge(sem.msg, 2)
-    for b in range(NBLK):
-        sc.dma_start(T.p[b * ROWS:(b + 1) * ROWS, :], T.box[b * ROWS:(b + 1) * ROWS, b, 0:R]).then_inc(sem.st_p, 16)
+    arrive = sorted(peers, key=lambda c: _order2(c, plan, T.cores, topo).index(core))
+    ve.wait_ge(sem.msg, nmsg)
+    prev = T.box[:, blk, R:2 * R]
+    for k, c in enumerate(arrive):
+        b = plan[c][1]
+        ve.wait_ge(sem["a2_%d" % b], len(eng))
+        if k > 0:
+            ve.wait_ge(sem.add, k)
+        if k < len(arrive) - 1:
+            ve.tensor_tensor(T.acc[:, k, :], prev, T.box[:, b, R:2 * R], AluOpType.add).then_inc(sem.add, 1)
+            prev = T.acc[:, k, :]
+        else:
+            ve.tensor_tensor(T.res[:], prev, T.box[:, b, R:2 * R], AluOpType.add).then_inc(sem.res, 1)
 
-    ve.wait_ge(sem.arr2, len(peers) * len(eng))
-    ve.wait_ge(sem.msg, 2)
-    src, base, n, nadd = T.box, 0, NBLK, 0
-    off = 0
-    while n > 2:
-        h = n // 2
-        ve.tensor_tensor(T.tmp[:, off:off + h, :], src[:, base:base + h, :], src[:, base + h:base + n, :],
-                         AluOpType.add).then_inc(sem.add, 1)
-        nadd += 1
-        ve.wait_ge(sem.add, nadd)
-        src, base, n = T.tmp, off, h
-        off += h
-    ve.tensor_tensor(T.res[:], src[:, base, :], src[:, base + 1, :], AluOpType.add).then_inc(sem.res, 1)
+    sc.wait_ge(sem.msg, nmsg)
+    sc.dma_start(T.p[lo:hi, :], T.box[0:ROWS, blk, 0:R]).then_inc(sem.st_p, 16)
+    for c in arrive:
+        b = plan[c][1]
+        sc.wait_ge(sem["a2_%d" % b], len(eng))
+        sc.dma_start(T.p[b * ROWS:(b + 1) * ROWS, :], T.box[0:ROWS, b, 0:R]).then_inc(sem.st_p, 16)
 
     sy.wait_ge(sem.res, 1)
-    sy.dma_start(T.q2[:], T.res[:, R:2 * R]).then_inc(sem.st_q, 16)
+    sy.dma_start(T.q2[:], T.res[:]).then_inc(sem.st_q, 16)
     sy.wait_ge(sem.st_q, 16)
     sc.wait_ge(sem.st_p, 16 * NBLK)
     g.wait_ge(sem.loc, nloc)

from concourse.bass import DstId, RemoteDMATransfer
from concourse.mybir import AluOpType

N = 16
D = 128
R = 16
NBLK = 4
NGRP = N // NBLK
ROWS = D // NBLK
PPS = D // N
J = ROWS // PPS
GP = NBLK * PPS
KB = (NGRP - 1) * GP
H = ROWS // 2

BF, F32 = "bfloat16", "float32"
SCRATCH = {
    "msend": ("dram", [NBLK, 128, ROWS], BF),
    "land": ("dram", [(NGRP - 1) * NBLK, 128, ROWS], BF),
    "big": ("sbuf", [128, J * D], BF),
    "mts": ("sbuf", [128, D], BF),
    "dir": ("sbuf", [128, NBLK, ROWS], BF),
    "z": ("sbuf", [N, ROWS * ROWS], BF),
    "sel": ("sbuf", [128, J * ROWS], BF),
    "idx": ("sbuf", [128, ROWS], BF),
    "iq": ("sbuf", [128, D + R], BF),
    "st": ("sbuf", [128, ROWS], BF),
    "sp": ("sbuf", [128, D + R], BF),
    "box": ("sbuf", [128, NBLK, 2 * R], BF),
    "acc": ("sbuf", [128, NBLK, R], F32),
    "res": ("sbuf", [128, R], BF),
    "ps_st": ("psum", [128, 512], F32),
    "ps_sp": ("psum", [128, 512], F32),
    "ps_c": ("psum", [128, 512], F32),
}
SEMAPHORES = (["ms", "mt", "q", "z", "idn", "idr", "idm", "sel", "big", "m_st", "c_st", "m_sp", "c_sp",
               "msg", "m_c", "add", "res", "st_p", "st_q", "loc"] + ["a1_%d" % k for k in range(NGRP)]
              + ["a2_%d" % k for k in range(NBLK)])


def _plan(cores, topo):
    chips = sorted({topo.chip(c) for c in cores})

    def far(a, b):
        return 0 if (topo.mates(a, b) or topo.same_plane(a, b)) else 1

    def match(rest):
        if len(rest) < 2:
            return (0, list(rest))
        best = None
        for b in rest[1:]:
            sub = match([y for y in rest[1:] if y != b])
            cost = sub[0] + far(rest[0], b)
            if best is None or cost < best[0]:
                best = (cost, [rest[0], b] + sub[1])
        return best

    seq = [c for ch in match(chips)[1] for c in sorted(cores) if topo.chip(c) == ch]
    return {c: (i // NBLK, i % NBLK) for i, c in enumerate(seq)}


def _bits(mask):
    return [e for e in range(mask.bit_length()) if (mask >> e) & 1]


def _m(engines):
    return sum(1 << e for e in engines)


def _dst(topo, c):
    rid, pid, _ = topo.addr(c)
    return DstId(rid=rid, pnc=pid)


def _order2(c, plan, cores, topo):
    peers = [x for x in cores if x != c and plan[x][0] == plan[c][0]]
    near = [x for x in peers if topo.chip(x) == topo.chip(c)]
    far = sorted(x for x in peers if topo.chip(x) != topo.chip(c))
    k = sorted([c] + near).index(c) % len(far)
    return near + far[k:] + far[:k]


def rank_program(g, core, T, topo):
    rank = T.rank_of(core)
    if rank is None:
        return
    sem = T.sem
    plan = _plan(T.cores, topo)
    grp, blk = plan[core]
    others = [c for c in T.cores if c != core]
    peers = [c for c in others if plan[c][0] == grp]
    near = [c for c in peers if topo.chip(c) == topo.chip(core)]
    far = [c for c in peers if topo.chip(c) != topo.chip(core)]
    lo, hi = blk * ROWS, (blk + 1) * ROWS
    pe, ve, sy, sc = g.tensor, g.vector, g.sync, g.scalar

    common = topo.mask(core, others[0])
    for c in others:
        common &= topo.mask(core, c)
    eng = _bits(common)
    ept = len(eng) // NBLK
    efar = len(eng) // len(far)

    h0 = H * sorted([core] + near).index(core)
    g.iota(T.idx[:, h0:h0 + H], [[-1, H]], -h0, 1, allow_small_or_imprecise_dtypes=True).then_inc(sem.idn, 1)
    g.wait_ge(sem.idn, 1)
    g.remote_dma_fused([RemoteDMATransfer(
        dst_ids=[_dst(topo, c) for c in near], dma_engine_mask=_m(eng), remote_sem=sem.idr,
        srcs=[T.idx[:, h0:h0 + H]], dsts=[T.idx[:, h0:h0 + H] for _ in near])], local_sem=sem.loc)
    nidr = len(eng)
    nloc = len(eng)

    sy.dma_start(T.msend[:], T.m[:]).then_inc(sem.ms, 16)
    sy.dma_start(T.mts[:], T.mt[:]).then_inc(sem.mt, 16)
    sc.dma_start(T.iq[:, D:D + R], T.q[:]).then_inc(sem.q, 16)
    ve.memset(T.z[:], 0.0).then_inc(sem.z, 1)
    ve.wait_ge(sem.z, 1)
    ve.memset(T.z[:, 0:ROWS * ROWS:ROWS + 1], 1.0).then_inc(sem.z, 1)
    sc.wait_ge(sem.z, 2)
    sc.dma_start(T.sel[:], T.z[:]).then_inc(sem.sel, 16)
    nmsg = 0
    a = ROWS
    while a < 128:
        n = a if 2 * a <= 128 else 128 - a
        ve.memset(T.box[a:a + n, blk, 0:R], 0.0).then_inc(sem.msg, 1)
        nmsg += 1
        a += n
    ve.wait_ge(sem.idn, 1)
    ve.wait_ge(sem.idr, nidr)
    for u in range(NBLK):
        ve.tensor_scalar(T.iq[:, u * ROWS:(u + 1) * ROWS], T.idx[:], float(u * ROWS), None,
                         AluOpType.is_equal).then_inc(sem.idm, 1)

    g.wait_ge(sem.ms, 16)
    trs = []
    for b in range(NBLK):
        own = sorted([c for c in others if plan[c][1] == b and plan[c][0] != grp],
                     key=lambda c: (plan[c][0] - grp - 1) % NGRP)
        trs.append(RemoteDMATransfer(
            dst_ids=[_dst(topo, c) for c in own], dma_engine_mask=_m(eng[b * ept:(b + 1) * ept]),
            remote_sem=sem["a1_%d" % grp], srcs=[T.msend[b]],
            dsts=[T.land[((plan[c][0] - grp - 1) % NGRP) * NBLK + blk] for c in own]))
    g.remote_dma_fused(trs, local_sem=sem.loc)
    nloc += NBLK * ept

    g.wait_ge(sem.mt, 16)
    trs = []
    for k, c in enumerate(far):
        b = plan[c][1]
        trs.append(RemoteDMATransfer(
            dst_ids=[_dst(topo, c)], dma_engine_mask=_m(eng[k * efar:(k + 1) * efar]), remote_sem=sem["a1_%d" % grp],
            srcs=[T.mts[:, b * ROWS:(b + 1) * ROWS]], dsts=[T.dir[:, blk, :]]))
    g.remote_dma_fused(trs, local_sem=sem.loc)
    for c in near:
        b = plan[c][1]
        g.remote_dma_fused([RemoteDMATransfer(
            dst_ids=[_dst(topo, c)], dma_engine_mask=_m(eng), remote_sem=sem["a1_%d" % grp],
            srcs=[T.mts[:, b * ROWS:(b + 1) * ROWS]], dsts=[T.dir[:, blk, :]])], local_sem=sem.loc)
    ndir = len(far) * efar + len(near) * len(eng)
    nloc += ndir

    for t in range(NGRP - 1):
        sg = (grp - 1 - t) % NGRP
        qu = sy if (NGRP - 2 - t) % 2 == 0 else sc
        qu.wait_ge(sem["a1_%d" % sg], NBLK * ept)
        qu.dma_start(T.big[t * GP:(t + 1) * GP, :], T.land[t * NBLK:(t + 1) * NBLK]).then_inc(sem.big, 16)

    pe.wait_ge(sem.idm, NBLK)
    pe.wait_ge(sem.mt, 16)
    pe.matmul(T.ps_st[:, 0:ROWS], lhsT=T.iq[:, 0:D], rhs=T.mts[:, lo:hi], start=True, stop=False)
    pe.wait_ge(sem["a1_%d" % grp], ndir)
    for c in peers:
        pe.matmul(T.ps_st[:, 0:ROWS], lhsT=T.iq[:, 0:D], rhs=T.dir[:, plan[c][1], :], start=False, stop=False)
    pe.wait_ge(sem.big, 16 * (NGRP - 1))
    pe.wait_ge(sem.sel, 16)
    for j in range(J):
        i = pe.matmul(T.ps_st[:, 0:ROWS], lhsT=T.big[0:KB, j * D:(j + 1) * D],
                      rhs=T.sel[0:KB, j * ROWS:(j + 1) * ROWS], start=False, stop=(j == J - 1))
    i.then_inc(sem.m_st, 1)
    ve.wait_ge(sem.m_st, 1)
    ve.tensor_copy(T.st[:], T.ps_st[:, 0:ROWS]).then_inc(sem.c_st, 1)

    pe.wait_ge(sem.c_st, 1)
    pe.wait_ge(sem.q, 16)
    pe.matmul(T.ps_sp[0:ROWS, 0:D + R], lhsT=T.st[:], rhs=T.iq[:], start=True, stop=True).then_inc(sem.m_sp, 1)
    ve.wait_ge(sem.m_sp, 1)
    ve.tensor_copy(T.sp[0:ROWS, :], T.ps_sp[0:ROWS, 0:D + R]).then_inc(sem.c_sp, 1)
    ve.tensor_copy(T.box[0:ROWS, blk, 0:R], T.ps_sp[0:ROWS, D:D + R]).then_inc(sem.msg, 1)
    nmsg += 1

    pe.wait_ge(sem.c_sp, 1)
    pe.matmul(T.ps_c[:, 0:R], lhsT=T.sp[0:ROWS, 0:D], rhs=T.sp[0:ROWS, D:D + R], start=True, stop=True).then_inc(
        sem.m_c, 1)
    ve.wait_ge(sem.m_c, 1)
    ve.tensor_copy(T.box[:, blk, R:2 * R], T.ps_c[:, 0:R]).then_inc(sem.msg, 1)
    nmsg += 1

    dests = _order2(core, plan, T.cores, topo)
    g.wait_ge(sem.msg, nmsg)
    g.remote_dma_fused([RemoteDMATransfer(
        dst_ids=[_dst(topo, c) for c in dests], dma_engine_mask=_m(eng), remote_sem=sem["a2_%d" % blk],
        srcs=[T.box[:, blk, :]], dsts=[T.box[:, blk, :] for _ in dests])], local_sem=sem.loc)
    nloc += len(eng)

    arrive = sorted(peers, key=lambda c: _order2(c, plan, T.cores, topo).index(core))
    ve.wait_ge(sem.msg, nmsg)
    prev = T.box[:, blk, R:2 * R]
    for k, c in enumerate(arrive):
        b = plan[c][1]
        ve.wait_ge(sem["a2_%d" % b], len(eng))
        if k > 0:
            ve.wait_ge(sem.add, k)
        if k < len(arrive) - 1:
            ve.tensor_tensor(T.acc[:, k, :], prev, T.box[:, b, R:2 * R], AluOpType.add).then_inc(sem.add, 1)
            prev = T.acc[:, k, :]
        else:
            ve.tensor_tensor(T.res[:], prev, T.box[:, b, R:2 * R], AluOpType.add).then_inc(sem.res, 1)

    sc.wait_ge(sem.msg, nmsg)
    sc.dma_start(T.p[lo:hi, :], T.box[0:ROWS, blk, 0:R]).then_inc(sem.st_p, 16)
    for c in arrive:
        b = plan[c][1]
        sc.wait_ge(sem["a2_%d" % b], len(eng))
        sc.dma_start(T.p[b * ROWS:(b + 1) * ROWS, :], T.box[0:ROWS, b, 0:R]).then_inc(sem.st_p, 16)

    sy.wait_ge(sem.res, 1)
    sy.dma_start(T.q2[:], T.res[:]).then_inc(sem.st_q, 16)
    sy.wait_ge(sem.st_q, 16)
    sc.wait_ge(sem.st_p, 16 * NBLK)
    g.wait_ge(sem.loc, nloc)
